import numpy as np
import ml_dtypes


def mxq(x, axis, fmt="e4m3"):
    dtype, down = {"e4m3": (ml_dtypes.float8_e4m3fn, 7), "e5m2": (ml_dtypes.float8_e5m2, 14)}[fmt]
    v = np.moveaxis(np.asarray(x, np.float32).astype(ml_dtypes.bfloat16).astype(np.float64), axis, -1)
    blocks = v.reshape(v.shape[:-1] + (-1, 32))
    amax = np.abs(blocks).max(-1, keepdims=True)
    byte = np.maximum(np.where(amax > 0, np.frexp(amax)[1] - 1 + 127, 0) - down, 1)
    scale = np.exp2(byte - 127.0)
    codes = (blocks / scale).astype(np.float32).astype(dtype).astype(np.float64)
    return np.moveaxis((codes * scale).reshape(v.shape), -1, axis)


WIDE = False


def mx_kscale(k):
    if not WIDE:
        return np.ones(k)
    levels = np.array([10, -10, 5, -5, 0])
    if k % 512:
        return np.exp2(np.random.permutation(np.resize(levels, k // 32))).repeat(32)
    a = np.empty((k // 512, 16))
    for p in range(k // 512):
        a[p, :8] = np.random.permutation(np.resize(levels, 8))
        for g in range(8):
            far = levels[np.abs(levels - a[p, g]) >= 10]
            a[p, g + 8] = far[np.random.randint(len(far))]
    return np.exp2(a.ravel()).repeat(32)


def f64(x):
    return np.asarray(x).astype(np.float64)


def striped(idx):
    return np.tile(idx.reshape(-1, 16).T, (8, 1)).astype(np.uint16)


def unstriped(offs):
    return offs[:16].T.reshape(-1).astype(np.int64)


def pack_weight(w):
    k, n = w.shape
    w = f64(np.asarray(w, np.float32).astype(ml_dtypes.bfloat16)).reshape(k // 32, 32, n)
    amax = np.abs(w).max(1)
    byte = np.clip(np.where(amax > 0, np.frexp(amax)[1] - 1 + 127 - 7, 1), 1, 254)
    scaled = (w * np.exp2(127.0 - byte)[:, None, :]).reshape(k, n).astype(np.float32)
    words = np.ascontiguousarray(scaled.reshape(k // 512, 128, 4, n).transpose(0, 1, 3, 2)).astype(ml_dtypes.float8_e4m3fn).view(np.uint8)
    return words, np.ascontiguousarray(byte.astype(np.uint8).reshape(k // 512, 16, n))


def unpack_weight(words, scales):
    g, p, n, _ = words.shape
    vals = np.ascontiguousarray(words).view(ml_dtypes.float8_e4m3fn).astype(np.float64) * np.repeat(np.exp2(scales.astype(np.float64) - 127.0), 8, axis=1)[..., None]
    return vals.transpose(0, 1, 3, 2).reshape(g * 512, n)


def sigmoid(v):
    return 1.0 / (1.0 + np.exp(-np.maximum(v, -700.0)))


K, T, S, V = 512, 2048, 512, 256


def setup_inputs():
    n = np.random.standard_normal
    s = mx_kscale(K)[:, None]
    packed_xT = pack_weight(n((K, T)) * s)
    return {
        "x_words": packed_xT[0],
        "x_scales": packed_xT[1],
        "hT": (n((K, V)) / np.sqrt(K) / s).astype(np.float32),
        "gT": (n((K, V)) / np.sqrt(K) / s).astype(np.float32),
        "fT": (n((K, V)) / np.sqrt(K) / s).astype(np.float32),
        "offs": striped(np.random.permutation(T)[:S]),
    }


def reference(x_words, x_scales, hT, gT, fT, offs):
    hTq = mxq(f64(hT), 0, "e4m3")
    xq = unpack_weight(x_words, x_scales)[:, unstriped(offs)]
    y = hTq.T @ xq
    e0 = np.exp(y)
    s0 = np.log(e0.sum(axis=1, keepdims=True))
    l0 = y - s0
    fTq = mxq(f64(fT), 0, "e4m3")
    ss = fTq.T @ xq
    e2 = np.exp(ss)
    s2 = np.log(e2.sum(axis=1, keepdims=True))
    l2 = ss - s2
    gTq = mxq(f64(gT), 0, "e4m3")
    z = gTq.T @ xq
    e1 = np.exp(z)
    s1 = np.log(e1.sum(axis=1, keepdims=True))
    l1 = z - s1
    p0 = np.exp(l0)
    p1 = np.exp(l1)
    m1 = np.log(0.5 * (p0 + p1))
    t1 = p0 * (l0 - m1) + p1 * (l1 - m1)
    j1 = t1.sum(axis=1, keepdims=True)
    p2 = np.exp(l2)
    m2 = np.log(0.5 * (p0 + p2))
    t2 = p0 * (l0 - m2) + p2 * (l2 - m2)
    j2 = t2.sum(axis=1, keepdims=True)
    ww = sigmoid(4.0 * (j1 - j2))
    return l0 - (l2 + (l1 - l2) * ww)

@@ -1,0 +1,231 @@
+import math
+from contextlib import ExitStack
+
+import concourse.mybir as mybir
+
+K, T, S, V = 512, 2048, 512, 256
+FLOPS = 3 * 2 * K * V * S
+
+F32 = mybir.dt.float32
+BF16 = mybir.dt.bfloat16
+I32 = mybir.dt.int32
+U32 = mybir.dt.uint32
+U16 = mybir.dt.uint16
+U8 = mybir.dt.uint8
+FP8X4 = mybir.dt.float8_e4m3fn_x4
+ALU = mybir.AluOpType
+ACT = mybir.ActivationFunctionType
+AX = mybir.AxisListType
+
+P = 128
+PACK = 4
+TILES = V // P
+EARLY, MIDDLE, LAST = 0, 1, 2
+
+
+def tile_picked_ydola_raw_p_kernel(tc, x_words, x_scales, hT, gT, fT, offs, out):
+    nc = tc.nc
+    with ExitStack() as ctx:
+        keep = ctx.enter_context(tc.tile_pool(name="keep", bufs=1))
+        psum = ctx.enter_context(tc.psum_pool(name="psum", bufs=1))
+
+        def col(layer, t):
+            return slice(TILES * layer + t, TILES * layer + t + 1)
+
+        def cols(first, last):
+            return slice(TILES * first, TILES * (last + 1))
+
+        offsets = keep.tile([P, S // 16], U16, name="offsets")
+        nc.sync.dma_start(offsets[:], offs)
+
+        table_scales = keep.tile([P, T], U8, name="table_scales", align_bytes=64)
+        landed_scales = keep.tile([P, T], U8, name="landed_scales", align_bytes=64)
+        nc.vector.memset(table_scales[:].bitcast(I32), 0)
+        for q in range(4):
+            rows = slice(32 * q, 32 * q + 4)
+            nc.sync.dma_start(
+                landed_scales[rows, :].bitcast(I32),
+                x_scales[0, 4 * q : 4 * q + 4, :].bitcast(I32),
+            )
+            nc.vector.tensor_copy(table_scales[rows, :].bitcast(I32), landed_scales[rows, :].bitcast(I32))
+
+        states = {LAST: hT, EARLY: gT, MIDDLE: fT}
+        raw = {}
+
+        def load_states(layer):
+            raw[layer] = keep.tile([P, PACK, V], F32, name=f"raw{layer}")
+            nc.sync.dma_start(raw[layer][:], states[layer].rearrange("(p j) c -> p j c", j=PACK))
+
+        load_states(LAST)
+        table_words = keep.tile([P, T], U32, name="table_words", align_bytes=64)
+        nc.sync.dma_start(
+            table_words[:].bitcast(I32),
+            x_words[0].rearrange("p n t -> p (n t)").bitcast(I32),
+        )
+        load_states(EARLY)
+        load_states(MIDDLE)
+
+        ones = keep.tile([P, 1], F32, name="ones")
+        base = keep.tile([P, 1], F32, name="base")
+        tiny = keep.tile([P, 1], F32, name="tiny")
+        minus_one = keep.tile([P, 1], F32, name="minus_one")
+        nc.gpsimd.memset(ones[:], 1.0)
+        nc.gpsimd.memset(tiny[:], 2.0**-60)
+        nc.gpsimd.memset(minus_one[:], -1.0)
+        nc.gpsimd.tensor_scalar(base[:], ones[:], math.exp(-4.0), 0.0, ALU.mult, ALU.add)
+
+        picked_scales = keep.tile([P, S], U8, name="picked_scales", align_bytes=64)
+        nc.vector.tensor_copy(picked_scales[:], table_scales[:].indirect(offsets[:]))
+
+        codes, scales = {}, {}
+
+        def quantise(layer, t):
+            grouped = keep.tile([P, P, PACK], BF16, name=f"grouped{layer}{t}", align_bytes=64)
+            src = raw[layer][:, :, t * P : (t + 1) * P]
+            if (layer, t) == (MIDDLE, TILES - 1):
+                nc.gpsimd.tensor_copy(grouped[:], src.rearrange("p j c -> p c j"))
+            else:
+                nc.scalar.activation(
+                    grouped[:].rearrange("p (c i) j -> p c j i", i=4),
+                    src.rearrange("p j (c i) -> p c j i", i=4),
+                    ACT.Copy,
+                )
+            codes[layer, t] = keep.tile([P, P], U32, name=f"codes{layer}{t}", align_bytes=64)
+            scales[layer, t] = keep.tile([P, P], U8, name=f"scales{layer}{t}", align_bytes=64)
+            nc.vector.quantize_mx(
+                out=codes[layer, t][:].bitcast(FP8X4),
+                scales=scales[layer, t][:],
+                in_=grouped[:].rearrange("p c j -> p (c j)"),
+            )
+
+        for t in range(TILES):
+            quantise(LAST, t)
+
+        picked_words = keep.tile([P, S], U32, name="picked_words", align_bytes=64)
+        nc.vector.tensor_copy(picked_words[:], table_words[:].indirect(offsets[:]))
+
+        neg_max = keep.tile([P, 3 * TILES], F32, name="neg_max")
+        total = keep.tile([P, 3 * TILES], F32, name="total")
+        inv_total = keep.tile([P, 3 * TILES], F32, name="inv_total")
+        logits, exps, neg_last = {}, {}, {}
+
+        def softmax_start(layer, t):
+            logits[layer, t] = psum.tile([P, S], F32, name=f"logits{layer}{t}")
+            nc.tensor.matmul_mx(
+                out=logits[layer, t][:],
+                lhsT=codes[layer, t][:].bitcast(FP8X4),
+                lhsT_scale=scales[layer, t][:],
+                rhs=picked_words[:].bitcast(FP8X4),
+                rhs_scale=picked_scales[:],
+                start=True,
+                stop=True,
+            )
+            if layer == LAST:
+                neg_last[t] = keep.tile([P, S], F32, name=f"neg_last{t}")
+                nc.vector.tensor_scalar(
+                    neg_last[t][:], logits[layer, t][:], -1.0, None, ALU.mult, ALU.min,
+                    accum_out=neg_max[:, col(layer, t)],
+                )
+            else:
+                nc.vector.tensor_reduce(neg_max[:, col(layer, t)], logits[layer, t][:], AX.X, ALU.max, negate=True)
+            exps[layer, t] = keep.tile([P, S], F32, name=f"exps{layer}{t}")
+            nc.scalar.activation(
+                exps[layer, t][:], logits[layer, t][:], ACT.Exp,
+                bias=neg_max[:, col(layer, t)], accum_out=total[:, col(layer, t)],
+            )
+
+        for t in range(TILES):
+            quantise(EARLY, t)
+            softmax_start(LAST, t)
+        for t in range(TILES):
+            quantise(MIDDLE, t)
+            softmax_start(EARLY, t)
+        nc.vector.reciprocal(inv_total[:, cols(LAST, LAST)], total[:, cols(LAST, LAST)])
+
+        mix = {}
+        for t in range(TILES):
+            scaled = keep.tile([P, S], F32, name=f"scaled{t}")
+            nc.gpsimd.tensor_scalar(
+                scaled[:], exps[LAST, t][:], total[:, col(EARLY, t)], inv_total[:, col(LAST, t)], ALU.mult, ALU.mult
+            )
+            mix[EARLY, t] = keep.tile([P, S], F32, name=f"mix{EARLY}{t}")
+            nc.gpsimd.tensor_tensor(mix[EARLY, t][:], scaled[:], exps[EARLY, t][:], ALU.add)
+
+        for t in range(TILES):
+            softmax_start(MIDDLE, t)
+
+        own = keep.tile([P, 2 * TILES], F32, name="own")
+        for layer in (EARLY, MIDDLE):
+            for t in range(TILES):
+                spent = keep.tile([P, S], F32, name=f"spent_own{layer}{t}")
+                nc.vector.scalar_tensor_tensor(
+                    spent[:], logits[layer, t][:], neg_max[:, col(layer, t)], exps[layer, t][:],
+                    ALU.add, ALU.mult, accum_out=own[:, col(layer, t)],
+                )
+
+        ratio = keep.tile([P, TILES], F32, name="ratio")
+        nc.vector.tensor_tensor(ratio[:], total[:, cols(MIDDLE, MIDDLE)], inv_total[:, cols(LAST, LAST)], ALU.mult)
+        nc.vector.reciprocal(inv_total[:, cols(EARLY, MIDDLE)], total[:, cols(EARLY, MIDDLE)])
+        for t in range(TILES):
+            mix[MIDDLE, t] = keep.tile([P, S], F32, name=f"mix{MIDDLE}{t}")
+            nc.vector.scalar_tensor_tensor(
+                mix[MIDDLE, t][:], exps[LAST, t][:], ratio[:, t : t + 1], exps[MIDDLE, t][:], ALU.mult, ALU.add
+            )
+
+        log_total = keep.tile([P, 3 * TILES], F32, name="log_total")
+        nc.scalar.activation(log_total[:], total[:], ACT.Ln)
+        lse = keep.tile([P, 3 * TILES], F32, name="lse")
+        nc.vector.tensor_tensor(lse[:], log_total[:], neg_max[:], ALU.subtract)
+        own_mean = keep.tile([P, 2 * TILES], F32, name="own_mean")
+        nc.vector.tensor_tensor(own_mean[:], own[:], inv_total[:, cols(EARLY, MIDDLE)], ALU.mult)
+        lse_step = keep.tile([P, 2 * TILES], F32, name="lse_step")
+        nc.vector.tensor_tensor(lse_step[:], lse[:, cols(EARLY, MIDDLE)], lse[:, cols(MIDDLE, LAST)], ALU.subtract)
+        own_term = keep.tile([P, 2 * TILES], F32, name="own_term")
+        nc.vector.tensor_tensor(own_term[:], own_mean[:], log_total[:, cols(EARLY, MIDDLE)], ALU.subtract)
+        own_gap = keep.tile([P, TILES], F32, name="own_gap")
+        nc.vector.tensor_tensor(
+            own_gap[:], own_term[:, cols(EARLY, EARLY)], own_term[:, cols(MIDDLE, MIDDLE)], ALU.subtract
+        )
+
+        mixed = keep.tile([P, 2 * TILES], F32, name="mixed")
+        weight = {}
+        for t in range(TILES):
+            for layer in (EARLY, MIDDLE):
+                log_mix = keep.tile([P, S], F32, name=f"log_mix{layer}{t}")
+                nc.scalar.activation(log_mix[:], mix[layer, t][:], ACT.Ln, bias=tiny[:], scale=inv_total[:, col(layer, t)])
+                spent = keep.tile([P, S], F32, name=f"spent_mix{layer}{t}")
+                nc.vector.scalar_tensor_tensor(
+                    spent[:], log_mix[:], inv_total[:, col(layer, t)], mix[layer, t][:],
+                    ALU.mult, ALU.mult, accum_out=mixed[:, col(layer, t)],
+                )
+            gap = keep.tile([P, 1], F32, name=f"gap{t}")
+            nc.vector.scalar_tensor_tensor(
+                gap[:], mixed[:, col(MIDDLE, t)], mixed[:, col(EARLY, t)], own_gap[:, t : t + 1],
+                ALU.subtract, ALU.add,
+            )
+            odds = keep.tile([P, 1], F32, name=f"odds{t}")
+            nc.gpsimd.tensor_tensor(odds[:], base[:], gap[:], ALU.pow)
+            weight[t] = odds
+
+        for t in range(TILES):
+            denom = keep.tile([P, 1], F32, name=f"denom{t}")
+            nc.vector.tensor_scalar(denom[:], weight[t][:], 1.0, None, ALU.add)
+            w = keep.tile([P, 1], F32, name=f"w{t}")
+            nc.vector.reciprocal(w[:], denom[:])
+            w_less_one = keep.tile([P, 1], F32, name=f"w_less_one{t}")
+            nc.scalar.activation(w_less_one[:], w[:], ACT.Identity, bias=minus_one[:])
+            shift = keep.tile([P, 1], F32, name=f"shift{t}")
+            nc.scalar.activation(
+                shift[:], w[:], ACT.Identity, scale=lse_step[:, col(EARLY, t)], bias=lse_step[:, col(MIDDLE, t)]
+            )
+            middle_part = keep.tile([P, S], F32, name=f"middle_part{t}")
+            nc.scalar.activation(
+                middle_part[:], logits[MIDDLE, t][:], ACT.Identity, scale=w_less_one[:], bias=shift[:]
+            )
+            early_part = keep.tile([P, S], F32, name=f"early_part{t}")
+            nc.vector.scalar_tensor_tensor(
+                early_part[:], logits[EARLY, t][:], w[:], neg_last[t][:], ALU.mult, ALU.add
+            )
+            result = keep.tile([P, S], F32, name=f"result{t}")
+            nc.vector.tensor_tensor(result[:], middle_part[:], early_part[:], ALU.subtract)
+            nc.sync.dma_start(out[t * P : (t + 1) * P, :], result[:])

@@ -1,4 +1,3 @@
-import math
 from contextlib import ExitStack
 
 import concourse.mybir as mybir
@@ -21,6 +20,7 @@ P = 128
 PACK = 4
 TILES = V // P
 EARLY, MIDDLE, LAST = 0, 1, 2
+SHARPNESS = 4.0
 
 
 def tile_picked_ydola_raw_p_kernel(tc, x_words, x_scales, hT, gT, fT, offs, out):
@@ -35,6 +35,14 @@ def tile_picked_ydola_raw_p_kernel(tc, x_words, x_scales, hT, gT, fT, offs, out)
         def cols(first, last):
             return slice(TILES * first, TILES * (last + 1))
 
+        states = {LAST: hT, EARLY: gT, MIDDLE: fT}
+        raw = {}
+
+        def load_states(layer):
+            raw[layer] = keep.tile([P, PACK, V], F32, name=f"raw{layer}")
+            nc.sync.dma_start(raw[layer][:], states[layer].rearrange("(p j) c -> p j c", j=PACK))
+
+        load_states(LAST)
         offsets = keep.tile([P, S // 16], U16, name="offsets")
         nc.sync.dma_start(offsets[:], offs)
 
@@ -49,30 +57,18 @@ def tile_picked_ydola_raw_p_kernel(tc, x_words, x_scales, hT, gT, fT, offs, out)
             )
             nc.vector.tensor_copy(table_scales[rows, :].bitcast(I32), landed_scales[rows, :].bitcast(I32))
 
-        states = {LAST: hT, EARLY: gT, MIDDLE: fT}
-        raw = {}
-
-        def load_states(layer):
-            raw[layer] = keep.tile([P, PACK, V], F32, name=f"raw{layer}")
-            nc.sync.dma_start(raw[layer][:], states[layer].rearrange("(p j) c -> p j c", j=PACK))
-
-        load_states(LAST)
+        load_states(EARLY)
         table_words = keep.tile([P, T], U32, name="table_words", align_bytes=64)
         nc.sync.dma_start(
             table_words[:].bitcast(I32),
             x_words[0].rearrange("p n t -> p (n t)").bitcast(I32),
         )
-        load_states(EARLY)
         load_states(MIDDLE)
 
         ones = keep.tile([P, 1], F32, name="ones")
-        base = keep.tile([P, 1], F32, name="base")
         tiny = keep.tile([P, 1], F32, name="tiny")
-        minus_one = keep.tile([P, 1], F32, name="minus_one")
         nc.gpsimd.memset(ones[:], 1.0)
         nc.gpsimd.memset(tiny[:], 2.0**-60)
-        nc.gpsimd.memset(minus_one[:], -1.0)
-        nc.gpsimd.tensor_scalar(base[:], ones[:], math.exp(-4.0), 0.0, ALU.mult, ALU.add)
 
         picked_scales = keep.tile([P, S], U8, name="picked_scales", align_bytes=64)
         nc.vector.tensor_copy(picked_scales[:], table_scales[:].indirect(offsets[:]))
@@ -82,14 +78,11 @@ def tile_picked_ydola_raw_p_kernel(tc, x_words, x_scales, hT, gT, fT, offs, out)
         def quantise(layer, t):
             grouped = keep.tile([P, P, PACK], BF16, name=f"grouped{layer}{t}", align_bytes=64)
             src = raw[layer][:, :, t * P : (t + 1) * P]
-            if (layer, t) == (MIDDLE, TILES - 1):
-                nc.gpsimd.tensor_copy(grouped[:], src.rearrange("p j c -> p c j"))
-            else:
-                nc.scalar.activation(
-                    grouped[:].rearrange("p (c i) j -> p c j i", i=4),
-                    src.rearrange("p j (c i) -> p c j i", i=4),
-                    ACT.Copy,
-                )
+            nc.scalar.activation(
+                grouped[:].rearrange("p (c i) j -> p c j i", i=4),
+                src.rearrange("p j (c i) -> p c j i", i=4),
+                ACT.Copy,
+            )
             codes[layer, t] = keep.tile([P, P], U32, name=f"codes{layer}{t}", align_bytes=64)
             scales[layer, t] = keep.tile([P, P], U8, name=f"scales{layer}{t}", align_bytes=64)
             nc.vector.quantize_mx(
@@ -98,11 +91,14 @@ def tile_picked_ydola_raw_p_kernel(tc, x_words, x_scales, hT, gT, fT, offs, out)
                 in_=grouped[:].rearrange("p c j -> p (c j)"),
             )
 
-        for t in range(TILES):
-            quantise(LAST, t)
+        for layer in (LAST, EARLY):
+            for t in range(TILES):
+                quantise(layer, t)
 
         picked_words = keep.tile([P, S], U32, name="picked_words", align_bytes=64)
         nc.vector.tensor_copy(picked_words[:], table_words[:].indirect(offsets[:]))
+        for t in range(TILES):
+            quantise(MIDDLE, t)
 
         neg_max = keep.tile([P, 3 * TILES], F32, name="neg_max")
         total = keep.tile([P, 3 * TILES], F32, name="total")
@@ -134,16 +130,11 @@ def tile_picked_ydola_raw_p_kernel(tc, x_words, x_scales, hT, gT, fT, offs, out)
                 bias=neg_max[:, col(layer, t)], accum_out=total[:, col(layer, t)],
             )
 
-        for t in range(TILES):
-            quantise(EARLY, t)
-            softmax_start(LAST, t)
-        for t in range(TILES):
-            quantise(MIDDLE, t)
-            softmax_start(EARLY, t)
-        nc.vector.reciprocal(inv_total[:, cols(LAST, LAST)], total[:, cols(LAST, LAST)])
-
         mix = {}
         for t in range(TILES):
+            softmax_start(LAST, t)
+            softmax_start(EARLY, t)
+            nc.vector.reciprocal(inv_total[:, col(LAST, t)], total[:, col(LAST, t)])
             scaled = keep.tile([P, S], F32, name=f"scaled{t}")
             nc.gpsimd.tensor_scalar(
                 scaled[:], exps[LAST, t][:], total[:, col(EARLY, t)], inv_total[:, col(LAST, t)], ALU.mult, ALU.mult
@@ -155,14 +146,16 @@ def tile_picked_ydola_raw_p_kernel(tc, x_words, x_scales, hT, gT, fT, offs, out)
             softmax_start(MIDDLE, t)
 
         own = keep.tile([P, 2 * TILES], F32, name="own")
-        for layer in (EARLY, MIDDLE):
-            for t in range(TILES):
-                spent = keep.tile([P, S], F32, name=f"spent_own{layer}{t}")
-                nc.vector.scalar_tensor_tensor(
-                    spent[:], logits[layer, t][:], neg_max[:, col(layer, t)], exps[layer, t][:],
-                    ALU.add, ALU.mult, accum_out=own[:, col(layer, t)],
-                )
 
+        def own_sum(layer, t):
+            spent = keep.tile([P, S], F32, name=f"spent_own{layer}{t}")
+            nc.vector.scalar_tensor_tensor(
+                spent[:], logits[layer, t][:], neg_max[:, col(layer, t)], exps[layer, t][:],
+                ALU.add, ALU.mult, accum_out=own[:, col(layer, t)],
+            )
+
+        for t in range(TILES):
+            own_sum(EARLY, t)
         ratio = keep.tile([P, TILES], F32, name="ratio")
         nc.vector.tensor_tensor(ratio[:], total[:, cols(MIDDLE, MIDDLE)], inv_total[:, cols(LAST, LAST)], ALU.mult)
         nc.vector.reciprocal(inv_total[:, cols(EARLY, MIDDLE)], total[:, cols(EARLY, MIDDLE)])
@@ -172,25 +165,32 @@ def tile_picked_ydola_raw_p_kernel(tc, x_words, x_scales, hT, gT, fT, offs, out)
                 mix[MIDDLE, t][:], exps[LAST, t][:], ratio[:, t : t + 1], exps[MIDDLE, t][:], ALU.mult, ALU.add
             )
 
+        for t in range(TILES):
+            own_sum(MIDDLE, t)
+
         log_total = keep.tile([P, 3 * TILES], F32, name="log_total")
         nc.scalar.activation(log_total[:], total[:], ACT.Ln)
         lse = keep.tile([P, 3 * TILES], F32, name="lse")
         nc.vector.tensor_tensor(lse[:], log_total[:], neg_max[:], ALU.subtract)
         own_mean = keep.tile([P, 2 * TILES], F32, name="own_mean")
-        nc.vector.tensor_tensor(own_mean[:], own[:], inv_total[:, cols(EARLY, MIDDLE)], ALU.mult)
+        nc.vector.scalar_tensor_tensor(
+            own_mean[:], own[:], SHARPNESS, inv_total[:, cols(EARLY, MIDDLE)], ALU.mult, ALU.mult
+        )
         lse_step = keep.tile([P, 2 * TILES], F32, name="lse_step")
-        nc.vector.tensor_tensor(lse_step[:], lse[:, cols(EARLY, MIDDLE)], lse[:, cols(MIDDLE, LAST)], ALU.subtract)
+        nc.vector.tensor_tensor(lse_step[:], lse[:, cols(MIDDLE, LAST)], lse[:, cols(EARLY, MIDDLE)], ALU.subtract)
         own_term = keep.tile([P, 2 * TILES], F32, name="own_term")
-        nc.vector.tensor_tensor(own_term[:], own_mean[:], log_total[:, cols(EARLY, MIDDLE)], ALU.subtract)
+        nc.vector.scalar_tensor_tensor(
+            own_term[:], log_total[:, cols(EARLY, MIDDLE)], -SHARPNESS, own_mean[:], ALU.mult, ALU.add
+        )
         own_gap = keep.tile([P, TILES], F32, name="own_gap")
         nc.vector.tensor_tensor(
             own_gap[:], own_term[:, cols(EARLY, EARLY)], own_term[:, cols(MIDDLE, MIDDLE)], ALU.subtract
         )
 
         mixed = keep.tile([P, 2 * TILES], F32, name="mixed")
-        weight = {}
-        for t in range(TILES):
-            for layer in (EARLY, MIDDLE):
+        known = keep.tile([P, TILES], F32, name="known")
+        for layer in (MIDDLE, EARLY):
+            for t in range(TILES):
                 log_mix = keep.tile([P, S], F32, name=f"log_mix{layer}{t}")
                 nc.scalar.activation(log_mix[:], mix[layer, t][:], ACT.Ln, bias=tiny[:], scale=inv_total[:, col(layer, t)])
                 spent = keep.tile([P, S], F32, name=f"spent_mix{layer}{t}")
@@ -198,34 +198,38 @@ def tile_picked_ydola_raw_p_kernel(tc, x_words, x_scales, hT, gT, fT, offs, out)
                     spent[:], log_mix[:], inv_total[:, col(layer, t)], mix[layer, t][:],
                     ALU.mult, ALU.mult, accum_out=mixed[:, col(layer, t)],
                 )
-            gap = keep.tile([P, 1], F32, name=f"gap{t}")
-            nc.vector.scalar_tensor_tensor(
-                gap[:], mixed[:, col(MIDDLE, t)], mixed[:, col(EARLY, t)], own_gap[:, t : t + 1],
-                ALU.subtract, ALU.add,
-            )
-            odds = keep.tile([P, 1], F32, name=f"odds{t}")
-            nc.gpsimd.tensor_tensor(odds[:], base[:], gap[:], ALU.pow)
-            weight[t] = odds
+            if layer == MIDDLE:
+                nc.vector.scalar_tensor_tensor(
+                    known[:], mixed[:, cols(MIDDLE, MIDDLE)], SHARPNESS, own_gap[:], ALU.mult, ALU.add
+                )
 
+        early_part, middle_part = {}, {}
         for t in range(TILES):
-            denom = keep.tile([P, 1], F32, name=f"denom{t}")
-            nc.vector.tensor_scalar(denom[:], weight[t][:], 1.0, None, ALU.add)
             w = keep.tile([P, 1], F32, name=f"w{t}")
-            nc.vector.reciprocal(w[:], denom[:])
-            w_less_one = keep.tile([P, 1], F32, name=f"w_less_one{t}")
-            nc.scalar.activation(w_less_one[:], w[:], ACT.Identity, bias=minus_one[:])
+            nc.scalar.activation(
+                w[:], mixed[:, col(EARLY, t)], ACT.Sigmoid, scale=-SHARPNESS, bias=known[:, t : t + 1]
+            )
+            rest = keep.tile([P, 1], F32, name=f"rest{t}")
+            nc.scalar.activation(rest[:], w[:], ACT.Identity, scale=-1.0, bias=ones[:])
             shift = keep.tile([P, 1], F32, name=f"shift{t}")
             nc.scalar.activation(
                 shift[:], w[:], ACT.Identity, scale=lse_step[:, col(EARLY, t)], bias=lse_step[:, col(MIDDLE, t)]
             )
-            middle_part = keep.tile([P, S], F32, name=f"middle_part{t}")
+            middle_part[t] = keep.tile([P, S], F32, name=f"middle_part{t}")
             nc.scalar.activation(
-                middle_part[:], logits[MIDDLE, t][:], ACT.Identity, scale=w_less_one[:], bias=shift[:]
+                middle_part[t][:], logits[MIDDLE, t][:], ACT.Identity, scale=rest[:], bias=shift[:]
             )
-            early_part = keep.tile([P, S], F32, name=f"early_part{t}")
+            early_part[t] = keep.tile([P, S], F32, name=f"early_part{t}")
             nc.vector.scalar_tensor_tensor(
-                early_part[:], logits[EARLY, t][:], w[:], neg_last[t][:], ALU.mult, ALU.add
+                early_part[t][:], logits[EARLY, t][:], w[:], neg_last[t][:], ALU.mult, ALU.add
             )
-            result = keep.tile([P, S], F32, name=f"result{t}")
-            nc.vector.tensor_tensor(result[:], middle_part[:], early_part[:], ALU.subtract)
-            nc.sync.dma_start(out[t * P : (t + 1) * P, :], result[:])
+        for t in range(TILES):
+            pieces = 2 if t == TILES - 1 else 1
+            width = S // pieces
+            for piece in range(pieces):
+                entries = slice(piece * width, (piece + 1) * width)
+                result = keep.tile([P, width], F32, name=f"result{t}{piece}")
+                nc.vector.scalar_tensor_tensor(
+                    result[:], early_part[t][:, entries], -1.0, middle_part[t][:, entries], ALU.mult, ALU.subtract
+                )
+                nc.sync.dma_start(out[t * P : (t + 1) * P, entries], result[:])

@@ -18,9 +18,14 @@ AX = mybir.AxisListType
 
 P = 128
 PACK = 4
+QUADRANT = 32
+LIST_ROWS = 16
+LINE = 4
 TILES = V // P
+HALF = S // 2
 EARLY, MIDDLE, LAST = 0, 1, 2
 SHARPNESS = 4.0
+TINY = 2.0**-60
 
 
 def tile_picked_ydola_raw_p_kernel(tc, x_words, x_scales, hT, gT, fT, offs, out):
@@ -32,8 +37,11 @@ def tile_picked_ydola_raw_p_kernel(tc, x_words, x_scales, hT, gT, fT, offs, out)
         def col(layer, t):
             return slice(TILES * layer + t, TILES * layer + t + 1)
 
-        def cols(first, last):
-            return slice(TILES * first, TILES * (last + 1))
+        def cols(first_layer, last_layer):
+            return slice(TILES * first_layer, TILES * (last_layer + 1))
+
+        def runs(tile):
+            return tile[:].rearrange("p (a b) -> p a b", a=PACK)
 
         states = {LAST: hT, EARLY: gT, MIDDLE: fT}
         raw = {}
@@ -43,32 +51,30 @@ def tile_picked_ydola_raw_p_kernel(tc, x_words, x_scales, hT, gT, fT, offs, out)
             nc.sync.dma_start(raw[layer][:], states[layer].rearrange("(p j) c -> p j c", j=PACK))
 
         load_states(LAST)
-        offsets = keep.tile([P, S // 16], U16, name="offsets")
+
+        offsets = keep.tile([P, S // LIST_ROWS], U16, name="offsets")
         nc.sync.dma_start(offsets[:], offs)
 
         table_scales = keep.tile([P, T], U8, name="table_scales", align_bytes=64)
-        landed_scales = keep.tile([P, T], U8, name="landed_scales", align_bytes=64)
-        nc.vector.memset(table_scales[:].bitcast(I32), 0)
-        for q in range(4):
-            rows = slice(32 * q, 32 * q + 4)
+        nc.gpsimd.memset(table_scales[:].bitcast(I32), 0)
+        for q in range(P // QUADRANT):
             nc.sync.dma_start(
-                landed_scales[rows, :].bitcast(I32),
-                x_scales[0, 4 * q : 4 * q + 4, :].bitcast(I32),
+                table_scales[QUADRANT * q : QUADRANT * q + PACK, :].bitcast(I32),
+                x_scales[0, PACK * q : PACK * (q + 1), :].bitcast(I32),
             )
-            nc.vector.tensor_copy(table_scales[rows, :].bitcast(I32), landed_scales[rows, :].bitcast(I32))
 
-        load_states(EARLY)
-        table_words = keep.tile([P, T], U32, name="table_words", align_bytes=64)
+        table_words = keep.tile([P, T], U32, name="table_words", tag="table_words", align_bytes=64)
         nc.sync.dma_start(
             table_words[:].bitcast(I32),
             x_words[0].rearrange("p n t -> p (n t)").bitcast(I32),
         )
+        load_states(EARLY)
         load_states(MIDDLE)
 
         ones = keep.tile([P, 1], F32, name="ones")
         tiny = keep.tile([P, 1], F32, name="tiny")
         nc.gpsimd.memset(ones[:], 1.0)
-        nc.gpsimd.memset(tiny[:], 2.0**-60)
+        nc.gpsimd.memset(tiny[:], TINY)
 
         picked_scales = keep.tile([P, S], U8, name="picked_scales", align_bytes=64)
         nc.vector.tensor_copy(picked_scales[:], table_scales[:].indirect(offsets[:]))
@@ -76,29 +82,40 @@ def tile_picked_ydola_raw_p_kernel(tc, x_words, x_scales, hT, gT, fT, offs, out)
         codes, scales = {}, {}
 
         def quantise(layer, t):
-            grouped = keep.tile([P, P, PACK], BF16, name=f"grouped{layer}{t}", align_bytes=64)
-            src = raw[layer][:, :, t * P : (t + 1) * P]
-            nc.scalar.activation(
-                grouped[:].rearrange("p (c i) j -> p c j i", i=4),
-                src.rearrange("p j (c i) -> p c j i", i=4),
-                ACT.Copy,
-            )
-            codes[layer, t] = keep.tile([P, P], U32, name=f"codes{layer}{t}", align_bytes=64)
-            scales[layer, t] = keep.tile([P, P], U8, name=f"scales{layer}{t}", align_bytes=64)
+            name = f"grouped{layer}{t}"
+            grouped = keep.tile([P, P, PACK], BF16, name=name, tag=name, align_bytes=64)
+            target = grouped[:].rearrange("p (c i) j -> p c j i", i=LINE)
+            source = raw[layer][:, :, t * P : (t + 1) * P].rearrange("p j (c i) -> p c j i", i=LINE)
+            if (layer, t) == (MIDDLE, TILES - 1):
+                nc.vector.tensor_copy(target, source)
+            else:
+                nc.scalar.activation(target, source, ACT.Copy)
+            name = f"codes{layer}{t}"
+            tag = "table_words" if (layer, t) == (LAST, 1) else name
+            codes[layer, t] = keep.tile([P, P], U32, name=name, tag=tag, align_bytes=64)
+            if (layer, t) == (EARLY, 0):
+                scales[layer, t] = scales[LAST, 1][PACK:P, :]
+            else:
+                scale_tile = keep.tile([P, P], U8, name=f"scales{layer}{t}", align_bytes=64)
+                scales[layer, t] = scale_tile[:]
             nc.vector.quantize_mx(
                 out=codes[layer, t][:].bitcast(FP8X4),
-                scales=scales[layer, t][:],
+                scales=scales[layer, t],
                 in_=grouped[:].rearrange("p c j -> p (c j)"),
             )
 
-        for layer in (LAST, EARLY):
-            for t in range(TILES):
-                quantise(layer, t)
+        quantise(LAST, 0)
 
         picked_words = keep.tile([P, S], U32, name="picked_words", align_bytes=64)
-        nc.vector.tensor_copy(picked_words[:], table_words[:].indirect(offsets[:]))
-        for t in range(TILES):
-            quantise(MIDDLE, t)
+        for half in range(2):
+            nc.vector.tensor_copy(
+                picked_words[:, half * HALF : (half + 1) * HALF],
+                table_words[:].indirect(offsets[:, half * HALF // LIST_ROWS : (half + 1) * HALF // LIST_ROWS]),
+            )
+        quantise(LAST, 1)
+        for layer in (EARLY, MIDDLE):
+            for t in range(TILES):
+                quantise(layer, t)
 
         neg_max = keep.tile([P, 3 * TILES], F32, name="neg_max")
         total = keep.tile([P, 3 * TILES], F32, name="total")
@@ -107,26 +124,34 @@ def tile_picked_ydola_raw_p_kernel(tc, x_words, x_scales, hT, gT, fT, offs, out)
 
         def softmax_start(layer, t):
             logits[layer, t] = psum.tile([P, S], F32, name=f"logits{layer}{t}")
-            nc.tensor.matmul_mx(
-                out=logits[layer, t][:],
-                lhsT=codes[layer, t][:].bitcast(FP8X4),
-                lhsT_scale=scales[layer, t][:],
-                rhs=picked_words[:].bitcast(FP8X4),
-                rhs_scale=picked_scales[:],
-                start=True,
-                stop=True,
-            )
+            width = HALF if (layer, t) == (LAST, 0) else S
+            for first in range(0, S, width):
+                entries = slice(first, first + width)
+                nc.tensor.matmul_mx(
+                    out=logits[layer, t][:, entries],
+                    lhsT=codes[layer, t][:].bitcast(FP8X4),
+                    lhsT_scale=scales[layer, t],
+                    rhs=picked_words[:, entries].bitcast(FP8X4),
+                    rhs_scale=picked_scales[:, entries],
+                    start=True,
+                    stop=True,
+                )
             if layer == LAST:
-                neg_last[t] = keep.tile([P, S], F32, name=f"neg_last{t}")
+                name = f"neg_last{t}"
+                tag = f"grouped{EARLY}{t}" if t == 0 else name
+                neg_last[t] = keep.tile([P, S], F32, name=name, tag=tag, align_bytes=64)
                 nc.vector.tensor_scalar(
                     neg_last[t][:], logits[layer, t][:], -1.0, None, ALU.mult, ALU.min,
                     accum_out=neg_max[:, col(layer, t)],
                 )
             else:
                 nc.vector.tensor_reduce(neg_max[:, col(layer, t)], logits[layer, t][:], AX.X, ALU.max, negate=True)
-            exps[layer, t] = keep.tile([P, S], F32, name=f"exps{layer}{t}")
+            if (layer, t) == (LAST, 0):
+                exps[layer, t] = raw[MIDDLE][:, :, 0:P]
+            else:
+                exps[layer, t] = runs(keep.tile([P, S], F32, name=f"exps{layer}{t}"))
             nc.scalar.activation(
-                exps[layer, t][:], logits[layer, t][:], ACT.Exp,
+                exps[layer, t], runs(logits[layer, t]), ACT.Exp,
                 bias=neg_max[:, col(layer, t)], accum_out=total[:, col(layer, t)],
             )
 
@@ -137,98 +162,102 @@ def tile_picked_ydola_raw_p_kernel(tc, x_words, x_scales, hT, gT, fT, offs, out)
             nc.vector.reciprocal(inv_total[:, col(LAST, t)], total[:, col(LAST, t)])
             scaled = keep.tile([P, S], F32, name=f"scaled{t}")
             nc.gpsimd.tensor_scalar(
-                scaled[:], exps[LAST, t][:], total[:, col(EARLY, t)], inv_total[:, col(LAST, t)], ALU.mult, ALU.mult
+                runs(scaled), exps[LAST, t], total[:, col(EARLY, t)], inv_total[:, col(LAST, t)], ALU.mult, ALU.mult
             )
             mix[EARLY, t] = keep.tile([P, S], F32, name=f"mix{EARLY}{t}")
-            nc.gpsimd.tensor_tensor(mix[EARLY, t][:], scaled[:], exps[EARLY, t][:], ALU.add)
+            nc.gpsimd.tensor_tensor(runs(mix[EARLY, t]), runs(scaled), exps[EARLY, t], ALU.add)
 
         for t in range(TILES):
             softmax_start(MIDDLE, t)
 
         own = keep.tile([P, 2 * TILES], F32, name="own")
+        for layer in (EARLY, MIDDLE):
+            for t in range(TILES):
+                own_products = keep.tile([P, S], F32, name=f"own_products{layer}{t}")
+                nc.vector.scalar_tensor_tensor(
+                    runs(own_products), runs(logits[layer, t]), neg_max[:, col(layer, t)], exps[layer, t],
+                    ALU.add, ALU.mult, accum_out=own[:, col(layer, t)],
+                )
 
-        def own_sum(layer, t):
-            spent = keep.tile([P, S], F32, name=f"spent_own{layer}{t}")
-            nc.vector.scalar_tensor_tensor(
-                spent[:], logits[layer, t][:], neg_max[:, col(layer, t)], exps[layer, t][:],
-                ALU.add, ALU.mult, accum_out=own[:, col(layer, t)],
-            )
-
-        for t in range(TILES):
-            own_sum(EARLY, t)
         ratio = keep.tile([P, TILES], F32, name="ratio")
         nc.vector.tensor_tensor(ratio[:], total[:, cols(MIDDLE, MIDDLE)], inv_total[:, cols(LAST, LAST)], ALU.mult)
         nc.vector.reciprocal(inv_total[:, cols(EARLY, MIDDLE)], total[:, cols(EARLY, MIDDLE)])
         for t in range(TILES):
             mix[MIDDLE, t] = keep.tile([P, S], F32, name=f"mix{MIDDLE}{t}")
             nc.vector.scalar_tensor_tensor(
-                mix[MIDDLE, t][:], exps[LAST, t][:], ratio[:, t : t + 1], exps[MIDDLE, t][:], ALU.mult, ALU.add
+                runs(mix[MIDDLE, t]), exps[LAST, t], ratio[:, t : t + 1], exps[MIDDLE, t], ALU.mult, ALU.add
             )
-
-        for t in range(TILES):
-            own_sum(MIDDLE, t)
 
         log_total = keep.tile([P, 3 * TILES], F32, name="log_total")
         nc.scalar.activation(log_total[:], total[:], ACT.Ln)
+
+        mixed = keep.tile([P, 2 * TILES], F32, name="mixed")
+
+        def mixed_sum(layer, t):
+            log_mix = keep.tile([P, S], F32, name=f"log_mix{layer}{t}")
+            nc.scalar.activation(
+                log_mix[:], mix[layer, t][:], ACT.Ln, bias=tiny[:], scale=inv_total[:, col(layer, t)]
+            )
+            mixed_products = keep.tile([P, S], F32, name=f"mixed_products{layer}{t}")
+            nc.vector.scalar_tensor_tensor(
+                mixed_products[:], log_mix[:], inv_total[:, col(layer, t)], mix[layer, t][:],
+                ALU.mult, ALU.mult, accum_out=mixed[:, col(layer, t)],
+            )
+
         lse = keep.tile([P, 3 * TILES], F32, name="lse")
         nc.vector.tensor_tensor(lse[:], log_total[:], neg_max[:], ALU.subtract)
         own_mean = keep.tile([P, 2 * TILES], F32, name="own_mean")
         nc.vector.scalar_tensor_tensor(
             own_mean[:], own[:], SHARPNESS, inv_total[:, cols(EARLY, MIDDLE)], ALU.mult, ALU.mult
         )
+        mixed_sum(EARLY, 0)
         lse_step = keep.tile([P, 2 * TILES], F32, name="lse_step")
         nc.vector.tensor_tensor(lse_step[:], lse[:, cols(MIDDLE, LAST)], lse[:, cols(EARLY, MIDDLE)], ALU.subtract)
         own_term = keep.tile([P, 2 * TILES], F32, name="own_term")
         nc.vector.scalar_tensor_tensor(
             own_term[:], log_total[:, cols(EARLY, MIDDLE)], -SHARPNESS, own_mean[:], ALU.mult, ALU.add
         )
+        mixed_sum(EARLY, 1)
         own_gap = keep.tile([P, TILES], F32, name="own_gap")
         nc.vector.tensor_tensor(
             own_gap[:], own_term[:, cols(EARLY, EARLY)], own_term[:, cols(MIDDLE, MIDDLE)], ALU.subtract
         )
-
-        mixed = keep.tile([P, 2 * TILES], F32, name="mixed")
+        mixed_sum(MIDDLE, 0)
         known = keep.tile([P, TILES], F32, name="known")
-        for layer in (MIDDLE, EARLY):
-            for t in range(TILES):
-                log_mix = keep.tile([P, S], F32, name=f"log_mix{layer}{t}")
-                nc.scalar.activation(log_mix[:], mix[layer, t][:], ACT.Ln, bias=tiny[:], scale=inv_total[:, col(layer, t)])
-                spent = keep.tile([P, S], F32, name=f"spent_mix{layer}{t}")
-                nc.vector.scalar_tensor_tensor(
-                    spent[:], log_mix[:], inv_total[:, col(layer, t)], mix[layer, t][:],
-                    ALU.mult, ALU.mult, accum_out=mixed[:, col(layer, t)],
-                )
-            if layer == MIDDLE:
-                nc.vector.scalar_tensor_tensor(
-                    known[:], mixed[:, cols(MIDDLE, MIDDLE)], SHARPNESS, own_gap[:], ALU.mult, ALU.add
-                )
+        nc.vector.scalar_tensor_tensor(
+            known[:], mixed[:, cols(EARLY, EARLY)], -SHARPNESS, own_gap[:], ALU.mult, ALU.add
+        )
+        mixed_sum(MIDDLE, 1)
 
+        weight = keep.tile([P, TILES], F32, name="weight")
+        rest = keep.tile([P, TILES], F32, name="rest")
+        shift = keep.tile([P, TILES], F32, name="shift")
+        for t in range(TILES):
+            nc.scalar.activation(
+                weight[:, t : t + 1], mixed[:, col(MIDDLE, t)], ACT.Sigmoid, scale=SHARPNESS, bias=known[:, t : t + 1]
+            )
+        for t in range(TILES):
+            nc.scalar.activation(rest[:, t : t + 1], weight[:, t : t + 1], ACT.Identity, scale=-1.0, bias=ones[:])
+            nc.scalar.activation(
+                shift[:, t : t + 1], weight[:, t : t + 1], ACT.Identity,
+                scale=lse_step[:, col(EARLY, t)], bias=lse_step[:, col(MIDDLE, t)],
+            )
         early_part, middle_part = {}, {}
         for t in range(TILES):
-            w = keep.tile([P, 1], F32, name=f"w{t}")
-            nc.scalar.activation(
-                w[:], mixed[:, col(EARLY, t)], ACT.Sigmoid, scale=-SHARPNESS, bias=known[:, t : t + 1]
-            )
-            rest = keep.tile([P, 1], F32, name=f"rest{t}")
-            nc.scalar.activation(rest[:], w[:], ACT.Identity, scale=-1.0, bias=ones[:])
-            shift = keep.tile([P, 1], F32, name=f"shift{t}")
-            nc.scalar.activation(
-                shift[:], w[:], ACT.Identity, scale=lse_step[:, col(EARLY, t)], bias=lse_step[:, col(MIDDLE, t)]
-            )
             middle_part[t] = keep.tile([P, S], F32, name=f"middle_part{t}")
             nc.scalar.activation(
-                middle_part[t][:], logits[MIDDLE, t][:], ACT.Identity, scale=rest[:], bias=shift[:]
+                middle_part[t][:], logits[MIDDLE, t][:], ACT.Identity,
+                scale=rest[:, t : t + 1], bias=shift[:, t : t + 1],
             )
             early_part[t] = keep.tile([P, S], F32, name=f"early_part{t}")
             nc.vector.scalar_tensor_tensor(
-                early_part[t][:], logits[EARLY, t][:], w[:], neg_last[t][:], ALU.mult, ALU.add
+                early_part[t][:], logits[EARLY, t][:], weight[:, t : t + 1], neg_last[t][:], ALU.mult, ALU.add
             )
         for t in range(TILES):
-            pieces = 2 if t == TILES - 1 else 1
-            width = S // pieces
-            for piece in range(pieces):
-                entries = slice(piece * width, (piece + 1) * width)
-                result = keep.tile([P, width], F32, name=f"result{t}{piece}")
+            width = HALF if t == TILES - 1 else S
+            for first in range(0, S, width):
+                entries = slice(first, first + width)
+                result = keep.tile([P, width], F32, name=f"result{t}_{first}")
                 nc.vector.scalar_tensor_tensor(
                     result[:], early_part[t][:, entries], -1.0, middle_part[t][:, entries], ALU.mult, ALU.subtract
                 )

from contextlib import ExitStack

import concourse.mybir as mybir

K, T, S, V = 512, 2048, 512, 256
FLOPS = 3 * 2 * K * V * S

F32 = mybir.dt.float32
BF16 = mybir.dt.bfloat16
I32 = mybir.dt.int32
U32 = mybir.dt.uint32
U16 = mybir.dt.uint16
U8 = mybir.dt.uint8
FP8X4 = mybir.dt.float8_e4m3fn_x4
ALU = mybir.AluOpType
ACT = mybir.ActivationFunctionType
AX = mybir.AxisListType

P = 128
PACK = 4
QUADRANT = 32
LIST_ROWS = 16
LINE = 4
TILES = V // P
HALF = S // 2
EARLY, MIDDLE, LAST = 0, 1, 2
SHARPNESS = 4.0
TINY = 2.0**-60


def tile_picked_ydola_raw_p_kernel(tc, x_words, x_scales, hT, gT, fT, offs, out):
    nc = tc.nc
    with ExitStack() as ctx:
        keep = ctx.enter_context(tc.tile_pool(name="keep", bufs=1))
        psum = ctx.enter_context(tc.psum_pool(name="psum", bufs=1))

        def col(layer, t):
            return slice(TILES * layer + t, TILES * layer + t + 1)

        def cols(first_layer, last_layer):
            return slice(TILES * first_layer, TILES * (last_layer + 1))

        def runs(tile):
            return tile[:].rearrange("p (a b) -> p a b", a=PACK)

        states = {LAST: hT, EARLY: gT, MIDDLE: fT}
        raw = {}

        def load_states(layer):
            raw[layer] = keep.tile([P, PACK, V], F32, name=f"raw{layer}")
            nc.sync.dma_start(raw[layer][:], states[layer].rearrange("(p j) c -> p j c", j=PACK))

        load_states(LAST)

        offsets = keep.tile([P, S // LIST_ROWS], U16, name="offsets")
        nc.sync.dma_start(offsets[:], offs)

        table_scales = keep.tile([P, T], U8, name="table_scales", align_bytes=64)
        nc.gpsimd.memset(table_scales[:].bitcast(I32), 0)
        for q in range(P // QUADRANT):
            nc.sync.dma_start(
                table_scales[QUADRANT * q : QUADRANT * q + PACK, :].bitcast(I32),
                x_scales[0, PACK * q : PACK * (q + 1), :].bitcast(I32),
            )

        table_words = keep.tile([P, T], U32, name="table_words", tag="table_words", align_bytes=64)
        nc.sync.dma_start(
            table_words[:].bitcast(I32),
            x_words[0].rearrange("p n t -> p (n t)").bitcast(I32),
        )
        load_states(EARLY)
        load_states(MIDDLE)

        ones = keep.tile([P, 1], F32, name="ones")
        tiny = keep.tile([P, 1], F32, name="tiny")
        nc.gpsimd.memset(ones[:], 1.0)
        nc.gpsimd.memset(tiny[:], TINY)

        picked_scales = keep.tile([P, S], U8, name="picked_scales", align_bytes=64)
        nc.vector.tensor_copy(picked_scales[:], table_scales[:].indirect(offsets[:]))

        codes, scales = {}, {}

        def quantise(layer, t):
            name = f"grouped{layer}{t}"
            grouped = keep.tile([P, P, PACK], BF16, name=name, tag=name, align_bytes=64)
            target = grouped[:].rearrange("p (c i) j -> p c j i", i=LINE)
            source = raw[layer][:, :, t * P : (t + 1) * P].rearrange("p j (c i) -> p c j i", i=LINE)
            if (layer, t) == (MIDDLE, TILES - 1):
                nc.vector.tensor_copy(target, source)
            else:
                nc.scalar.activation(target, source, ACT.Copy)
            name = f"codes{layer}{t}"
            tag = "table_words" if (layer, t) == (LAST, 1) else name
            codes[layer, t] = keep.tile([P, P], U32, name=name, tag=tag, align_bytes=64)
            if (layer, t) == (EARLY, 0):
                scales[layer, t] = scales[LAST, 1][PACK:P, :]
            else:
                scale_tile = keep.tile([P, P], U8, name=f"scales{layer}{t}", align_bytes=64)
                scales[layer, t] = scale_tile[:]
            nc.vector.quantize_mx(
                out=codes[layer, t][:].bitcast(FP8X4),
                scales=scales[layer, t],
                in_=grouped[:].rearrange("p c j -> p (c j)"),
            )

        quantise(LAST, 0)

        picked_words = keep.tile([P, S], U32, name="picked_words", align_bytes=64)
        for half in range(2):
            nc.vector.tensor_copy(
                picked_words[:, half * HALF : (half + 1) * HALF],
                table_words[:].indirect(offsets[:, half * HALF // LIST_ROWS : (half + 1) * HALF // LIST_ROWS]),
            )
        quantise(LAST, 1)
        for layer in (EARLY, MIDDLE):
            for t in range(TILES):
                quantise(layer, t)

        neg_max = keep.tile([P, 3 * TILES], F32, name="neg_max")
        total = keep.tile([P, 3 * TILES], F32, name="total")
        inv_total = keep.tile([P, 3 * TILES], F32, name="inv_total")
        logits, exps, neg_last = {}, {}, {}

        def softmax_start(layer, t):
            logits[layer, t] = psum.tile([P, S], F32, name=f"logits{layer}{t}")
            width = HALF if (layer, t) == (LAST, 0) else S
            for first in range(0, S, width):
                entries = slice(first, first + width)
                nc.tensor.matmul_mx(
                    out=logits[layer, t][:, entries],
                    lhsT=codes[layer, t][:].bitcast(FP8X4),
                    lhsT_scale=scales[layer, t],
                    rhs=picked_words[:, entries].bitcast(FP8X4),
                    rhs_scale=picked_scales[:, entries],
                    start=True,
                    stop=True,
                )
            if layer == LAST:
                name = f"neg_last{t}"
                tag = f"grouped{EARLY}{t}" if t == 0 else name
                neg_last[t] = keep.tile([P, S], F32, name=name, tag=tag, align_bytes=64)
                nc.vector.tensor_scalar(
                    neg_last[t][:], logits[layer, t][:], -1.0, None, ALU.mult, ALU.min,
                    accum_out=neg_max[:, col(layer, t)],
                )
            else:
                nc.vector.tensor_reduce(neg_max[:, col(layer, t)], logits[layer, t][:], AX.X, ALU.max, negate=True)
            if (layer, t) == (LAST, 0):
                exps[layer, t] = raw[MIDDLE][:, :, 0:P]
            else:
                exps[layer, t] = runs(keep.tile([P, S], F32, name=f"exps{layer}{t}"))
            nc.scalar.activation(
                exps[layer, t], runs(logits[layer, t]), ACT.Exp,
                bias=neg_max[:, col(layer, t)], accum_out=total[:, col(layer, t)],
            )

        mix = {}
        for t in range(TILES):
            softmax_start(LAST, t)
            softmax_start(EARLY, t)
            nc.vector.reciprocal(inv_total[:, col(LAST, t)], total[:, col(LAST, t)])
            scaled = keep.tile([P, S], F32, name=f"scaled{t}")
            nc.gpsimd.tensor_scalar(
                runs(scaled), exps[LAST, t], total[:, col(EARLY, t)], inv_total[:, col(LAST, t)], ALU.mult, ALU.mult
            )
            mix[EARLY, t] = keep.tile([P, S], F32, name=f"mix{EARLY}{t}")
            nc.gpsimd.tensor_tensor(runs(mix[EARLY, t]), runs(scaled), exps[EARLY, t], ALU.add)

        for t in range(TILES):
            softmax_start(MIDDLE, t)

        own = keep.tile([P, 2 * TILES], F32, name="own")
        for layer in (EARLY, MIDDLE):
            for t in range(TILES):
                own_products = keep.tile([P, S], F32, name=f"own_products{layer}{t}")
                nc.vector.scalar_tensor_tensor(
                    runs(own_products), runs(logits[layer, t]), neg_max[:, col(layer, t)], exps[layer, t],
                    ALU.add, ALU.mult, accum_out=own[:, col(layer, t)],
                )

        ratio = keep.tile([P, TILES], F32, name="ratio")
        nc.vector.tensor_tensor(ratio[:], total[:, cols(MIDDLE, MIDDLE)], inv_total[:, cols(LAST, LAST)], ALU.mult)
        nc.vector.reciprocal(inv_total[:, cols(EARLY, MIDDLE)], total[:, cols(EARLY, MIDDLE)])
        for t in range(TILES):
            mix[MIDDLE, t] = keep.tile([P, S], F32, name=f"mix{MIDDLE}{t}")
            nc.vector.scalar_tensor_tensor(
                runs(mix[MIDDLE, t]), exps[LAST, t], ratio[:, t : t + 1], exps[MIDDLE, t], ALU.mult, ALU.add
            )

        log_total = keep.tile([P, 3 * TILES], F32, name="log_total")
        nc.scalar.activation(log_total[:], total[:], ACT.Ln)

        mixed = keep.tile([P, 2 * TILES], F32, name="mixed")

        def mixed_sum(layer, t):
            log_mix = keep.tile([P, S], F32, name=f"log_mix{layer}{t}")
            nc.scalar.activation(
                log_mix[:], mix[layer, t][:], ACT.Ln, bias=tiny[:], scale=inv_total[:, col(layer, t)]
            )
            mixed_products = keep.tile([P, S], F32, name=f"mixed_products{layer}{t}")
            nc.vector.scalar_tensor_tensor(
                mixed_products[:], log_mix[:], inv_total[:, col(layer, t)], mix[layer, t][:],
                ALU.mult, ALU.mult, accum_out=mixed[:, col(layer, t)],
            )

        lse = keep.tile([P, 3 * TILES], F32, name="lse")
        nc.vector.tensor_tensor(lse[:], log_total[:], neg_max[:], ALU.subtract)
        own_mean = keep.tile([P, 2 * TILES], F32, name="own_mean")
        nc.vector.scalar_tensor_tensor(
            own_mean[:], own[:], SHARPNESS, inv_total[:, cols(EARLY, MIDDLE)], ALU.mult, ALU.mult
        )
        mixed_sum(EARLY, 0)
        lse_step = keep.tile([P, 2 * TILES], F32, name="lse_step")
        nc.vector.tensor_tensor(lse_step[:], lse[:, cols(MIDDLE, LAST)], lse[:, cols(EARLY, MIDDLE)], ALU.subtract)
        own_term = keep.tile([P, 2 * TILES], F32, name="own_term")
        nc.vector.scalar_tensor_tensor(
            own_term[:], log_total[:, cols(EARLY, MIDDLE)], -SHARPNESS, own_mean[:], ALU.mult, ALU.add
        )
        mixed_sum(EARLY, 1)
        own_gap = keep.tile([P, TILES], F32, name="own_gap")
        nc.vector.tensor_tensor(
            own_gap[:], own_term[:, cols(EARLY, EARLY)], own_term[:, cols(MIDDLE, MIDDLE)], ALU.subtract
        )
        mixed_sum(MIDDLE, 0)
        known = keep.tile([P, TILES], F32, name="known")
        nc.vector.scalar_tensor_tensor(
            known[:], mixed[:, cols(EARLY, EARLY)], -SHARPNESS, own_gap[:], ALU.mult, ALU.add
        )
        mixed_sum(MIDDLE, 1)

        weight = keep.tile([P, TILES], F32, name="weight")
        rest = keep.tile([P, TILES], F32, name="rest")
        shift = keep.tile([P, TILES], F32, name="shift")
        for t in range(TILES):
            nc.scalar.activation(
                weight[:, t : t + 1], mixed[:, col(MIDDLE, t)], ACT.Sigmoid, scale=SHARPNESS, bias=known[:, t : t + 1]
            )
        for t in range(TILES):
            nc.scalar.activation(rest[:, t : t + 1], weight[:, t : t + 1], ACT.Identity, scale=-1.0, bias=ones[:])
            nc.scalar.activation(
                shift[:, t : t + 1], weight[:, t : t + 1], ACT.Identity,
                scale=lse_step[:, col(EARLY, t)], bias=lse_step[:, col(MIDDLE, t)],
            )
        early_part, middle_part = {}, {}
        for t in range(TILES):
            middle_part[t] = keep.tile([P, S], F32, name=f"middle_part{t}")
            nc.scalar.activation(
                middle_part[t][:], logits[MIDDLE, t][:], ACT.Identity,
                scale=rest[:, t : t + 1], bias=shift[:, t : t + 1],
            )
            early_part[t] = keep.tile([P, S], F32, name=f"early_part{t}")
            nc.vector.scalar_tensor_tensor(
                early_part[t][:], logits[EARLY, t][:], weight[:, t : t + 1], neg_last[t][:], ALU.mult, ALU.add
            )
        for t in range(TILES):
            width = HALF if t == TILES - 1 else S
            for first in range(0, S, width):
                entries = slice(first, first + width)
                result = keep.tile([P, width], F32, name=f"result{t}_{first}")
                nc.vector.scalar_tensor_tensor(
                    result[:], early_part[t][:, entries], -1.0, middle_part[t][:, entries], ALU.mult, ALU.subtract
                )
                nc.sync.dma_start(out[t * P : (t + 1) * P, entries], result[:])
